import numpy as np, ml_dtypes
CORES = [16,23,24,31,64,71]
N = 6
KB, QP = 1, 128
def setup_inputs(rng):
    q = rng.standard_normal((N, 128, QP), dtype=np.float32) / 4; k = rng.standard_normal((N, 128, KB * 128), dtype=np.float32)
    a = 2 * np.pi * rng.random((N, QP)); s = 400 * rng.random((N, QP)) ** 1.5; q[:, 0, :] = s * np.cos(a); q[:, 1, :] = s * np.sin(a); q[:, 2, :] = 150 * rng.standard_normal((N, QP)); k[:, 2, :] = 1 + k[:, 2, :] / 50
    a = (2 * np.pi * rng.random() + np.pi / 2 * (rng.permutation(N).reshape(N, 1, 1) + 0.5) / N - 0.5 + (np.arange(KB).reshape(1, KB, 1) + rng.random((N, KB, 128))) / KB).reshape(N, KB * 128); k[:, 0, :] = np.cos(a); k[:, 1, :] = np.sin(a)
    return {"q": q.astype(ml_dtypes.bfloat16), "k": k.astype(ml_dtypes.bfloat16), "v": rng.standard_normal((N, 128, KB * 128), dtype=np.float32).astype(ml_dtypes.bfloat16)}
def setup_inputs_big(rng):
    d = setup_inputs(rng)
    for k in ("v",): d[k] = (d[k].astype(np.float32) * 1048576.0).astype(d[k].dtype)
    return d
def setup_inputs_small(rng):
    d = setup_inputs(rng)
    for k in ("v",): d[k] = (d[k].astype(np.float32) * (1 / 1048576.0)).astype(d[k].dtype)
    return d
def reference(q, k, v):
    Q, K, V = q.astype(np.float64), k.astype(np.float64), v.astype(np.float64)
    y = np.zeros((N, QP, 128))
    for r in range(N):
        js = list(range(N))
        S = np.concatenate([K[j].T @ Q[r] for j in js], axis=0)
        P = np.exp(S - S.max(axis=0)); P = P / P.sum(axis=0)
        y[r] = P.T @ np.concatenate([V[j][:, 128 * b:128 * b + 128] for j in js for b in range(KB)], axis=0)
    return {"y": y.astype(ml_dtypes.bfloat16)}

@@ -1,0 +1,207 @@
+from concourse.bass import DstId, RemoteDMATransfer
+from concourse.mybir import AluOpType, AxisListType, ActivationFunctionType
+
+NS = 3
+W = 128
+_STAGE_SEMS = ["st%da", "st%db", "mx%d", "nm%d", "ex%da", "ex%db", "w%d", "tp%da", "tp%db", "pt%da", "pt%db",
+               "dg%d", "x%d", "la%d", "pv%d", "ev%d"]
+
+SCRATCH = {
+    "kv": ("sbuf", [128, NS * 4 * W], "bfloat16"),
+    "qs": ("sbuf", [128, W], "bfloat16"),
+    "ones": ("sbuf", [128, W], "bfloat16"),
+    "idn": ("sbuf", [128, W], "bfloat16"),
+    "p": ("sbuf", [128, NS * 2 * W], "bfloat16"),
+    "pt": ("sbuf", [128, NS * 2 * W], "bfloat16"),
+    "dg": ("sbuf", [128, NS * W], "bfloat16"),
+    "osb": ("sbuf", [128, NS * W], "bfloat16"),
+    "col": ("sbuf", [128, 8 * (NS + 1)], "float32"),
+    "ys": ("sbuf", [128, W], "bfloat16"),
+    "sta": ("psum", [128, 512], "float32"),
+    "stb": ("psum", [128, 512], "float32"),
+    "tpa": ("psum", [128, 1024], "bfloat16"),
+    "tpb": ("psum", [128, 1024], "bfloat16"),
+    "o0": ("psum", [128, 512], "float32"),
+    "o1": ("psum", [128, 512], "float32"),
+}
+SEMAPHORES = (["ld", "ldq", "one", "idn", "pa", "snt", "rc", "yy", "out"] + ["b%d" % c for c in range(NS)]
+              + [n % s for s in range(NS) for n in _STAGE_SEMS])
+
+
+def _bits(mask):
+    return [e for e in range(mask.bit_length()) if (mask >> e) & 1]
+
+
+def _plan(T, topo):
+    cores = list(T.cores)
+    chips = []
+    for c in cores:
+        if topo.chip(c) not in chips:
+            chips.append(topo.chip(c))
+    members = [[c for c in cores if topo.chip(c) == ch] for ch in chips]
+    jobs = []
+    for a in range(len(chips)):
+        for b in range(len(chips)):
+            if a != b:
+                elig = [c for c in members[a] if all(topo.may_write(c, d) for d in members[b])]
+                jobs.append((len(elig), a, b, elig))
+    jobs.sort(key=lambda j: j[:3])
+    sends = {c: [] for c in cores}
+    sender = {}
+    for _, a, b, elig in jobs:
+        s = min(elig, key=lambda c: len(sends[c]))
+        sends[s] = sends[s] + members[b]
+        sender[(a, b)] = s
+    return chips, members, sends, sender
+
+
+def rank_program(g, core, T, topo):
+    rank = T.rank_of(core)
+    if rank is None:
+        return
+    sem = T.sem
+    chips, members, sends, sender = _plan(T, topo)
+    slot = chips.index(topo.chip(core))
+    pos = members[slot].index(core)
+    partner = members[slot][1 - pos]
+
+    def kcol(c, b):
+        return c * 4 * W + W + b * W
+
+    def vcol(c, b):
+        return c * 4 * W + 3 * b * W
+
+    common = topo.mask(core, partner)
+    for d in T.cores:
+        if d != core:
+            common &= topo.mask(core, d)
+    eng = _bits(common)
+    n1 = len(eng)
+
+    def share(s):
+        return len(eng) // len(sends[s])
+
+    g.sync.dma_start(T.kv[:, kcol(slot, pos):kcol(slot, pos) + W], T.k[:, :]).then_inc(sem.ld, 16)
+    g.scalar.dma_start(T.kv[:, vcol(slot, pos):vcol(slot, pos) + W], T.v[:, :]).then_inc(sem.ld, 16)
+    g.sync.dma_start(T.qs[:, :], T.q[:, :]).then_inc(sem.ldq, 16)
+
+    g.vector.memset(T.ones[:, :], 1.0).then_inc(sem.one, 1)
+    g.wait_ge(sem.one, 1)
+    g.affine_select(T.idn[:, :], T.ones[:, :], [[-1, W]], AluOpType.is_equal, 0.0, 0, 1).then_inc(sem.idn, 1)
+
+    h0 = slot * 4 * W + pos * 2 * W
+    rid, pid, _ = topo.addr(partner)
+    g.wait_ge(sem.ld, 32)
+    g.remote_dma(T.kv[:, h0:h0 + 2 * W], T.kv[:, h0:h0 + 2 * W], sem.pa, sem.snt, pid, rid, common)
+    sent = n1
+
+    if sends[core]:
+        g.wait_ge(sem.pa, n1)
+        per = share(core)
+        b0 = slot * 4 * W
+        trs = []
+        for i, d in enumerate(sends[core]):
+            rid, pid, _ = topo.addr(d)
+            m = 0
+            for e in eng[i * per:(i + 1) * per]:
+                m |= 1 << e
+            trs.append(RemoteDMATransfer(dst_ids=[DstId(rid=rid, pnc=pid)], dma_engine_mask=m,
+                                         remote_sem=sem["b%d" % slot], src=T.kv[:, b0:b0 + 4 * W],
+                                         dst=T.kv[:, b0:b0 + 4 * W]))
+            sent += per
+        g.remote_dma_fused(trs, local_sem=sem.snt)
+    g.wait_ge(sem.snt, sent)
+
+    def late(c):
+        direct = topo.mates(chips[c], chips[slot]) or topo.same_plane(chips[c], chips[slot])
+        return (len(sends[sender[(c, slot)]]), 0 if direct else 1)
+
+    order = [slot] + sorted([c for c in range(len(chips)) if c != slot], key=late)
+    pe, dve, act = g.tensor, g.vector, g.scalar
+    ST = [T.sta, T.stb]
+    TP = [T.tpa, T.tpb]
+    OB = [T.o0, T.o1]
+    AB = "ab"
+    X = AxisListType.X
+
+    def col(i):
+        return T.col[:, i:i + 1]
+
+    pe.wait_ge(sem.ld, 32)
+    pe.wait_ge(sem.ldq, 16)
+    pe.wait_ge(sem.pa, n1)
+    pe.wait_ge(sem.idn, 1)
+    dve.wait_ge(sem.idn, 1)
+    for s, c in enumerate(order):
+        last = s == NS - 1
+        cb = 8 * s
+        negm = col(cb + 8)
+        O = OB[s % 2][:, 0:W]
+
+        def S(n, s=s):
+            return sem[n % s]
+
+        if s > 0:
+            pe.wait_ge(sem["b%d" % c], share(sender[(c, slot)]))
+        for b in range(2):
+            pe.matmul(ST[b][:, 0:W], T.qs[:, :], T.kv[:, kcol(c, b):kcol(c, b) + W], True, True).then_inc(
+                S("st%d" + AB[b]), 1)
+        for b in range(2):
+            dve.wait_ge(S("st%d" + AB[b]), 1)
+            dve.tensor_reduce(col(cb + 1 + b), ST[b][:, 0:W], X, AluOpType.max, negate=True).then_inc(S("mx%d"), 1)
+        dve.wait_ge(S("mx%d"), 2)
+        if s > 0:
+            dve.wait_ge(sem["nm%d" % (s - 1)], 1)
+        lo = cb if s > 0 else cb + 1
+        dve.tensor_reduce(negm, T.col[:, lo:cb + 3], X, AluOpType.min).then_inc(S("nm%d"), 1)
+        act.wait_ge(S("nm%d"), 1)
+        for b in range(2):
+            pc = (2 * s + b) * W
+            act.activation(T.p[:, pc:pc + W], ST[b][:, 0:W], ActivationFunctionType.Exp, bias=negm, scale=1.0,
+                           accum_out=col(cb + 4 + b)).then_inc(S("ex%d" + AB[b]), 1)
+        if s > 0:
+            act.activation(col(cb + 6), col(cb), ActivationFunctionType.Exp, bias=negm, scale=-1.0).then_inc(
+                S("w%d"), 1)
+        for b in range(2):
+            pc = (2 * s + b) * W
+            pe.wait_ge(S("ex%d" + AB[b]), 1)
+            pe.transpose(TP[b][:, 0:W], T.p[:, pc:pc + W], T.idn[:, :]).then_inc(S("tp%d" + AB[b]), 1)
+        dve.wait_ge(S("tp%da"), 1)
+        dve.tensor_copy(T.pt[:, 2 * s * W:(2 * s + 1) * W], TP[0][:, 0:W]).then_inc(S("pt%da"), 1)
+        if s > 0:
+            dve.wait_ge(S("w%d"), 1)
+            dve.tensor_scalar(T.dg[:, s * W:(s + 1) * W], T.idn[:, :], col(cb + 6), None, AluOpType.mult).then_inc(
+                S("dg%d"), 1)
+            dve.wait_ge(sem["la%d" % (s - 1)], 1)
+            dve.tensor_tensor(col(cb + 3), col(cb - 1), col(cb + 6), AluOpType.mult).then_inc(S("x%d"), 1)
+        dve.wait_ge(S("tp%db"), 1)
+        dve.tensor_copy(T.pt[:, (2 * s + 1) * W:(2 * s + 2) * W], TP[1][:, 0:W]).then_inc(S("pt%db"), 1)
+        npv = 2
+        if s > 0:
+            pe.wait_ge(S("dg%d"), 1)
+            pe.wait_ge(sem["ev%d" % (s - 1)], 1)
+            pe.matmul(O, T.dg[:, s * W:(s + 1) * W], T.osb[:, (s - 1) * W:s * W], True, False).then_inc(S("pv%d"), 1)
+            npv = 3
+        for b in range(2):
+            pe.wait_ge(S("pt%d" + AB[b]), 1)
+            pe.matmul(O, T.pt[:, (2 * s + b) * W:(2 * s + b + 1) * W], T.kv[:, vcol(c, b):vcol(c, b) + W],
+                      s == 0 and b == 0, b == 1).then_inc(S("pv%d"), 1)
+        dve.wait_ge(S("ex%da"), 1)
+        dve.wait_ge(S("ex%db"), 1)
+        if s > 0:
+            dve.wait_ge(S("x%d"), 1)
+        dve.tensor_reduce(col(cb + 7), T.col[:, (cb + 3 if s > 0 else cb + 4):cb + 6], X, AluOpType.add).then_inc(
+            S("la%d"), 1)
+        if not last:
+            dve.wait_ge(S("pv%d"), npv)
+            dve.tensor_copy(T.osb[:, s * W:(s + 1) * W], O).then_inc(S("ev%d"), 1)
+        else:
+            dve.wait_ge(S("la%d"), 1)
+            dve.reciprocal(col(cb + 9), col(cb + 7)).then_inc(sem.rc, 1)
+            dve.wait_ge(sem.rc, 1)
+            dve.wait_ge(S("pv%d"), npv)
+            dve.tensor_scalar(T.ys[:, :], O, col(cb + 9), None, AluOpType.mult).then_inc(sem.yy, 1)
+
+    g.sync.wait_ge(sem.yy, 1)
+    g.sync.dma_start(T.y[:, :], T.ys[:, :]).then_inc(sem.out, 16)
+    g.sync.wait_ge(sem.out, 16)

@@ -1,35 +1,54 @@
 from concourse.bass import DstId, RemoteDMATransfer
 from concourse.mybir import AluOpType, AxisListType, ActivationFunctionType
 
-NS = 3
+NC = 3
+NS = 2
+NB = 4
 W = 128
-_STAGE_SEMS = ["st%da", "st%db", "mx%d", "nm%d", "ex%da", "ex%db", "w%d", "tp%da", "tp%db", "pt%da", "pt%db",
-               "dg%d", "x%d", "la%d", "pv%d", "ev%d"]
+NCORES = 80
 
 SCRATCH = {
-    "kv": ("sbuf", [128, NS * 4 * W], "bfloat16"),
+    "kv": ("sbuf", [128, NC * 4 * W], "bfloat16"),
     "qs": ("sbuf", [128, W], "bfloat16"),
     "ones": ("sbuf", [128, W], "bfloat16"),
     "idn": ("sbuf", [128, W], "bfloat16"),
-    "p": ("sbuf", [128, NS * 2 * W], "bfloat16"),
-    "pt": ("sbuf", [128, NS * 2 * W], "bfloat16"),
-    "dg": ("sbuf", [128, NS * W], "bfloat16"),
-    "osb": ("sbuf", [128, NS * W], "bfloat16"),
-    "col": ("sbuf", [128, 8 * (NS + 1)], "float32"),
+    "p": ("sbuf", [128, NC * 2 * W], "bfloat16"),
+    "pt": ("sbuf", [128, NC * 2 * W], "bfloat16"),
+    "dg": ("sbuf", [128, W], "bfloat16"),
+    "osb": ("sbuf", [128, W], "bfloat16"),
+    "col": ("sbuf", [128, 16 * (NS + 1)], "float32"),
     "ys": ("sbuf", [128, W], "bfloat16"),
-    "sta": ("psum", [128, 512], "float32"),
-    "stb": ("psum", [128, 512], "float32"),
+    "st0": ("psum", [128, 512], "float32"),
+    "st1": ("psum", [128, 512], "float32"),
+    "st2": ("psum", [128, 512], "float32"),
+    "st3": ("psum", [128, 512], "float32"),
     "tpa": ("psum", [128, 1024], "bfloat16"),
     "tpb": ("psum", [128, 1024], "bfloat16"),
     "o0": ("psum", [128, 512], "float32"),
     "o1": ("psum", [128, 512], "float32"),
 }
-SEMAPHORES = (["ld", "ldq", "one", "idn", "pa", "snt", "rc", "yy", "out"] + ["b%d" % c for c in range(NS)]
-              + [n % s for s in range(NS) for n in _STAGE_SEMS])
+SEMAPHORES = (["ld", "ldq", "one", "idn", "pa", "snt", "rc", "yy", "out"] + ["b%d" % c for c in range(NC)]
+              + ["%s%d" % (n, s) for s in range(NS) for n in ("mx", "nm", "w", "dg", "x", "la", "pv", "ev")]
+              + ["%s%d_%d" % (n, s, b) for s in range(NS) for b in range(NB) for n in ("st", "ex", "tp", "pt")])
 
 
 def _bits(mask):
     return [e for e in range(mask.bit_length()) if (mask >> e) & 1]
+
+
+def _mask(engs):
+    m = 0
+    for e in engs:
+        m |= 1 << e
+    return m
+
+
+def _common(x, T, topo):
+    m = -1
+    for d in T.cores:
+        if d != x:
+            m = topo.mask(x, d) if m < 0 else m & topo.mask(x, d)
+    return _bits(m)
 
 
 def _plan(T, topo):
@@ -44,25 +63,79 @@ def _plan(T, topo):
         for b in range(len(chips)):
             if a != b:
                 elig = [c for c in members[a] if all(topo.may_write(c, d) for d in members[b])]
-                jobs.append((len(elig), a, b, elig))
-    jobs.sort(key=lambda j: j[:3])
+                near = topo.mates(chips[a], chips[b]) or topo.same_plane(chips[a], chips[b])
+                jobs.append((len(elig), 1 if near else 0, a, b, elig))
+    jobs.sort(key=lambda j: j[:4])
     sends = {c: [] for c in cores}
+    relay = {}
+    feeds = {c: [] for c in cores}
     sender = {}
-    for _, a, b, elig in jobs:
+    for _, _, a, b, elig in jobs:
         s = min(elig, key=lambda c: len(sends[c]))
+        if sends[s]:
+            free = [c for c in range(NCORES) if topo.chip(c) == chips[a] and c not in cores and c not in relay
+                    and all(topo.may_write(c, d) for d in members[b])]
+            free.sort(key=lambda c: (topo.die(c) == topo.die(s), c))
+            free = free[:len(members[a])]
+            if len(free) == len(members[a]):
+                for owner, h in zip(members[a], free):
+                    relay[h] = (owner, members[b])
+                    feeds[owner] = feeds[owner] + [h]
+                sender[(a, b)] = free
+                continue
         sends[s] = sends[s] + members[b]
-        sender[(a, b)] = s
-    return chips, members, sends, sender
+        sender[(a, b)] = [s]
+    return chips, members, sends, sender, relay, feeds
+
+
+def _step1(x, partner, feeds, T, topo):
+    dests = [partner] + feeds[x]
+    eng = _common(x, T, topo)
+    m = topo.mask(x, partner)
+    for d in dests:
+        m &= topo.mask(x, d)
+    pool = eng + [e for e in _bits(m) if e not in eng]
+    per = 1
+    while per * 2 * len(dests) <= len(pool) and per * 2 <= len(eng):
+        per *= 2
+    return [(d, pool[i * per:(i + 1) * per]) for i, d in enumerate(dests)]
 
 
 def rank_program(g, core, T, topo):
     rank = T.rank_of(core)
-    if rank is None:
-        return
     sem = T.sem
-    chips, members, sends, sender = _plan(T, topo)
-    slot = chips.index(topo.chip(core))
-    pos = members[slot].index(core)
+    chips, members, sends, sender, relay, feeds = _plan(T, topo)
+
+    def place(c):
+        s = chips.index(topo.chip(c))
+        return s, members[s].index(c)
+
+    def per_dest(x):
+        return len(_common(x, T, topo)) // len(sends[x] if x in sends else relay[x][1])
+
+    def cross(dests, c0, c1, bsem):
+        eng = _common(core, T, topo)
+        per = per_dest(core)
+        trs = []
+        for i, d in enumerate(dests):
+            rid, pid, _ = topo.addr(d)
+            trs.append(RemoteDMATransfer(dst_ids=[DstId(rid=rid, pnc=pid)],
+                                         dma_engine_mask=_mask(eng[i * per:(i + 1) * per]), remote_sem=bsem,
+                                         src=T.kv[:, c0:c1], dst=T.kv[:, c0:c1]))
+        g.remote_dma_fused(trs, local_sem=sem.snt)
+        return per * len(dests)
+
+    if rank is None:
+        if core in relay:
+            owner, dests = relay[core]
+            oslot, opos = place(owner)
+            got = [e for d, e in _step1(owner, members[oslot][1 - opos], feeds, T, topo) if d == core][0]
+            h0 = oslot * 4 * W + opos * 2 * W
+            g.wait_ge(sem.pa, len(got))
+            g.wait_ge(sem.snt, cross(dests, h0, h0 + 2 * W, sem["b%d" % oslot]))
+        return
+
+    slot, pos = place(core)
     partner = members[slot][1 - pos]
 
     def kcol(c, b):
@@ -71,15 +144,7 @@ def rank_program(g, core, T, topo):
     def vcol(c, b):
         return c * 4 * W + 3 * b * W
 
-    common = topo.mask(core, partner)
-    for d in T.cores:
-        if d != core:
-            common &= topo.mask(core, d)
-    eng = _bits(common)
-    n1 = len(eng)
-
-    def share(s):
-        return len(eng) // len(sends[s])
+    n1 = len(_step1(partner, core, feeds, T, topo)[0][1])
 
     g.sync.dma_start(T.kv[:, kcol(slot, pos):kcol(slot, pos) + W], T.k[:, :]).then_inc(sem.ld, 16)
     g.scalar.dma_start(T.kv[:, vcol(slot, pos):vcol(slot, pos) + W], T.v[:, :]).then_inc(sem.ld, 16)
@@ -90,39 +155,34 @@ def rank_program(g, core, T, topo):
     g.affine_select(T.idn[:, :], T.ones[:, :], [[-1, W]], AluOpType.is_equal, 0.0, 0, 1).then_inc(sem.idn, 1)
 
     h0 = slot * 4 * W + pos * 2 * W
-    rid, pid, _ = topo.addr(partner)
     g.wait_ge(sem.ld, 32)
-    g.remote_dma(T.kv[:, h0:h0 + 2 * W], T.kv[:, h0:h0 + 2 * W], sem.pa, sem.snt, pid, rid, common)
-    sent = n1
+    trs = []
+    sent = 0
+    for d, engs in _step1(core, partner, feeds, T, topo):
+        rid, pid, _ = topo.addr(d)
+        trs.append(RemoteDMATransfer(dst_ids=[DstId(rid=rid, pnc=pid)], dma_engine_mask=_mask(engs),
+                                     remote_sem=sem.pa, src=T.kv[:, h0:h0 + 2 * W], dst=T.kv[:, h0:h0 + 2 * W]))
+        sent += len(engs)
+    g.remote_dma_fused(trs, local_sem=sem.snt)
 
     if sends[core]:
         g.wait_ge(sem.pa, n1)
-        per = share(core)
         b0 = slot * 4 * W
-        trs = []
-        for i, d in enumerate(sends[core]):
-            rid, pid, _ = topo.addr(d)
-            m = 0
-            for e in eng[i * per:(i + 1) * per]:
-                m |= 1 << e
-            trs.append(RemoteDMATransfer(dst_ids=[DstId(rid=rid, pnc=pid)], dma_engine_mask=m,
-                                         remote_sem=sem["b%d" % slot], src=T.kv[:, b0:b0 + 4 * W],
-                                         dst=T.kv[:, b0:b0 + 4 * W]))
-            sent += per
-        g.remote_dma_fused(trs, local_sem=sem.snt)
+        sent += cross(sends[core], b0, b0 + 4 * W, sem["b%d" % slot])
     g.wait_ge(sem.snt, sent)
 
     def late(c):
-        direct = topo.mates(chips[c], chips[slot]) or topo.same_plane(chips[c], chips[slot])
-        return (len(sends[sender[(c, slot)]]), 0 if direct else 1)
+        near = topo.mates(chips[c], chips[slot]) or topo.same_plane(chips[c], chips[slot])
+        return (0 if sender[(c, slot)][0] in sends else 1, 0 if near else 1)
 
-    order = [slot] + sorted([c for c in range(len(chips)) if c != slot], key=late)
+    foreign = sorted([c for c in range(len(chips)) if c != slot], key=late)
+    stages = [[(slot, 0), (slot, 1)], [(c, h) for c in foreign for h in range(2)]]
     pe, dve, act = g.tensor, g.vector, g.scalar
-    ST = [T.sta, T.stb]
+    ST = [T.st0, T.st1, T.st2, T.st3]
     TP = [T.tpa, T.tpb]
     OB = [T.o0, T.o1]
-    AB = "ab"
     X = AxisListType.X
+    Exp = ActivationFunctionType.Exp
 
     def col(i):
         return T.col[:, i:i + 1]
@@ -132,75 +192,102 @@ def rank_program(g, core, T, topo):
     pe.wait_ge(sem.pa, n1)
     pe.wait_ge(sem.idn, 1)
     dve.wait_ge(sem.idn, 1)
-    for s, c in enumerate(order):
+    first = 0
+    for s, blocks in enumerate(stages):
+        nb = len(blocks)
         last = s == NS - 1
-        cb = 8 * s
-        negm = col(cb + 8)
-        O = OB[s % 2][:, 0:W]
+        cb = 16 * s
+        negm = col(cb + 16)
+        O = OB[s][:, 0:W]
 
-        def S(n, s=s):
-            return sem[n % s]
+        def S(n, b=None, s=s):
+            return sem["%s%d" % (n, s)] if b is None else sem["%s%d_%d" % (n, s, b)]
 
-        if s > 0:
-            pe.wait_ge(sem["b%d" % c], share(sender[(c, slot)]))
-        for b in range(2):
-            pe.matmul(ST[b][:, 0:W], T.qs[:, :], T.kv[:, kcol(c, b):kcol(c, b) + W], True, True).then_inc(
-                S("st%d" + AB[b]), 1)
-        for b in range(2):
-            dve.wait_ge(S("st%d" + AB[b]), 1)
-            dve.tensor_reduce(col(cb + 1 + b), ST[b][:, 0:W], X, AluOpType.max, negate=True).then_inc(S("mx%d"), 1)
-        dve.wait_ge(S("mx%d"), 2)
+        def blk(buf, b, first=first):
+            return buf[:, (first + b) * W:(first + b + 1) * W]
+
+        seen = slot
+        for b, (c, h) in enumerate(blocks):
+            if c != seen:
+                pe.wait_ge(sem["b%d" % c], sum(per_dest(x) for x in sender[(c, slot)]))
+                seen = c
+            pe.matmul(ST[b][:, 0:W], T.qs[:, :], T.kv[:, kcol(c, h):kcol(c, h) + W], True, True).then_inc(
+                S("st", b), 1)
+        for b in range(nb):
+            dve.wait_ge(S("st", b), 1)
+            dve.tensor_reduce(col(cb + 1 + b), ST[b][:, 0:W], X, AluOpType.max, negate=True).then_inc(S("mx"), 1)
+        dve.wait_ge(S("mx"), nb)
         if s > 0:
             dve.wait_ge(sem["nm%d" % (s - 1)], 1)
-        lo = cb if s > 0 else cb + 1
-        dve.tensor_reduce(negm, T.col[:, lo:cb + 3], X, AluOpType.min).then_inc(S("nm%d"), 1)
-        act.wait_ge(S("nm%d"), 1)
-        for b in range(2):
-            pc = (2 * s + b) * W
-            act.activation(T.p[:, pc:pc + W], ST[b][:, 0:W], ActivationFunctionType.Exp, bias=negm, scale=1.0,
-                           accum_out=col(cb + 4 + b)).then_inc(S("ex%d" + AB[b]), 1)
+        dve.tensor_reduce(negm, T.col[:, (cb if s > 0 else cb + 1):cb + 1 + nb], X, AluOpType.min).then_inc(
+            S("nm"), 1)
+        act.wait_ge(S("nm"), 1)
         if s > 0:
-            act.activation(col(cb + 6), col(cb), ActivationFunctionType.Exp, bias=negm, scale=-1.0).then_inc(
-                S("w%d"), 1)
-        for b in range(2):
-            pc = (2 * s + b) * W
-            pe.wait_ge(S("ex%d" + AB[b]), 1)
-            pe.transpose(TP[b][:, 0:W], T.p[:, pc:pc + W], T.idn[:, :]).then_inc(S("tp%d" + AB[b]), 1)
-        dve.wait_ge(S("tp%da"), 1)
-        dve.tensor_copy(T.pt[:, 2 * s * W:(2 * s + 1) * W], TP[0][:, 0:W]).then_inc(S("pt%da"), 1)
+            act.activation(col(cb + 10), col(cb), Exp, bias=negm, scale=-1.0).then_inc(S("w"), 1)
+        for b in range(nb):
+            act.activation(blk(T.p, b), ST[b][:, 0:W], Exp, bias=negm, scale=1.0,
+                           accum_out=col(cb + 6 + b)).then_inc(S("ex", b), 1)
         if s > 0:
-            dve.wait_ge(S("w%d"), 1)
-            dve.tensor_scalar(T.dg[:, s * W:(s + 1) * W], T.idn[:, :], col(cb + 6), None, AluOpType.mult).then_inc(
-                S("dg%d"), 1)
+            dve.wait_ge(S("w"), 1)
+            dve.tensor_scalar(T.dg[:, :], T.idn[:, :], col(cb + 10), None, AluOpType.mult).then_inc(S("dg"), 1)
             dve.wait_ge(sem["la%d" % (s - 1)], 1)
-            dve.tensor_tensor(col(cb + 3), col(cb - 1), col(cb + 6), AluOpType.mult).then_inc(S("x%d"), 1)
-        dve.wait_ge(S("tp%db"), 1)
-        dve.tensor_copy(T.pt[:, (2 * s + 1) * W:(2 * s + 2) * W], TP[1][:, 0:W]).then_inc(S("pt%db"), 1)
-        npv = 2
+            dve.tensor_tensor(col(cb + 5), col(cb - 16 + 11), col(cb + 10), AluOpType.mult).then_inc(S("x"), 1)
+
+        npv = nb
         if s > 0:
-            pe.wait_ge(S("dg%d"), 1)
+            pe.wait_ge(S("dg"), 1)
             pe.wait_ge(sem["ev%d" % (s - 1)], 1)
-            pe.matmul(O, T.dg[:, s * W:(s + 1) * W], T.osb[:, (s - 1) * W:s * W], True, False).then_inc(S("pv%d"), 1)
-            npv = 3
-        for b in range(2):
-            pe.wait_ge(S("pt%d" + AB[b]), 1)
-            pe.matmul(O, T.pt[:, (2 * s + b) * W:(2 * s + b + 1) * W], T.kv[:, vcol(c, b):vcol(c, b) + W],
-                      s == 0 and b == 0, b == 1).then_inc(S("pv%d"), 1)
-        dve.wait_ge(S("ex%da"), 1)
-        dve.wait_ge(S("ex%db"), 1)
-        if s > 0:
-            dve.wait_ge(S("x%d"), 1)
-        dve.tensor_reduce(col(cb + 7), T.col[:, (cb + 3 if s > 0 else cb + 4):cb + 6], X, AluOpType.add).then_inc(
-            S("la%d"), 1)
+            pe.matmul(O, T.dg[:, :], T.osb[:, :], True, False).then_inc(S("pv"), 1)
+            npv += 1
+
+        def turn(b):
+            pe.wait_ge(S("ex", b), 1)
+            if b >= 2:
+                pe.wait_ge(S("pt", b - 2), 1)
+            pe.transpose(TP[b % 2][:, 0:W], blk(T.p, b), T.idn[:, :]).then_inc(S("tp", b), 1)
+
+        turn(0)
+        turn(1)
+        for b, (c, h) in enumerate(blocks):
+            pe.wait_ge(S("pt", b), 1)
+            pe.matmul(O, blk(T.pt, b), T.kv[:, vcol(c, h):vcol(c, h) + W], s == 0 and b == 0,
+                      b == nb - 1).then_inc(S("pv"), 1)
+            if b + 2 < nb:
+                turn(b + 2)
+
+        def copy(b):
+            dve.wait_ge(S("tp", b), 1)
+            dve.tensor_copy(blk(T.pt, b), TP[b % 2][:, 0:W]).then_inc(S("pt", b), 1)
+
+        def rowsum():
+            for b in range(nb):
+                dve.wait_ge(S("ex", b), 1)
+            if s > 0:
+                dve.wait_ge(S("x"), 1)
+            dve.tensor_reduce(col(cb + 11), T.col[:, (cb + 5 if s > 0 else cb + 6):cb + 6 + nb], X,
+                              AluOpType.add).then_inc(S("la"), 1)
+
+        def recip():
+            dve.wait_ge(S("la"), 1)
+            dve.reciprocal(col(cb + 12), col(cb + 11)).then_inc(sem.rc, 1)
+
         if not last:
-            dve.wait_ge(S("pv%d"), npv)
-            dve.tensor_copy(T.osb[:, s * W:(s + 1) * W], O).then_inc(S("ev%d"), 1)
+            for b in range(nb):
+                copy(b)
+            rowsum()
+            dve.wait_ge(S("pv"), npv)
+            dve.tensor_copy(T.osb[:, :], O).then_inc(S("ev"), 1)
         else:
-            dve.wait_ge(S("la%d"), 1)
-            dve.reciprocal(col(cb + 9), col(cb + 7)).then_inc(sem.rc, 1)
+            for b in range(nb - 2):
+                copy(b)
+            rowsum()
+            copy(nb - 2)
+            recip()
+            copy(nb - 1)
             dve.wait_ge(sem.rc, 1)
-            dve.wait_ge(S("pv%d"), npv)
-            dve.tensor_scalar(T.ys[:, :], O, col(cb + 9), None, AluOpType.mult).then_inc(sem.yy, 1)
+            dve.wait_ge(S("pv"), npv)
+            dve.tensor_scalar(T.ys[:, :], O, col(cb + 12), None, AluOpType.mult).then_inc(sem.yy, 1)
+        first += nb
 
     g.sync.wait_ge(sem.yy, 1)
     g.sync.dma_start(T.y[:, :], T.ys[:, :]).then_inc(sem.out, 16)

@@ -2,9 +2,8 @@ from concourse.bass import DstId, RemoteDMATransfer
 from concourse.mybir import AluOpType, AxisListType, ActivationFunctionType
 
 NC = 3
-NS = 2
-NB = 4
 W = 128
+H = 64
 NCORES = 80
 
 SCRATCH = {
@@ -16,7 +15,9 @@ SCRATCH = {
     "pt": ("sbuf", [128, NC * 2 * W], "bfloat16"),
     "dg": ("sbuf", [128, W], "bfloat16"),
     "osb": ("sbuf", [128, W], "bfloat16"),
-    "col": ("sbuf", [128, 16 * (NS + 1)], "float32"),
+    "t1": ("sbuf", [128, W], "bfloat16"),
+    "osa": ("sbuf", [128, W], "bfloat16"),
+    "col": ("sbuf", [128, 48], "float32"),
     "ys": ("sbuf", [128, W], "bfloat16"),
     "st0": ("psum", [128, 512], "float32"),
     "st1": ("psum", [128, 512], "float32"),
@@ -27,9 +28,11 @@ SCRATCH = {
     "o0": ("psum", [128, 512], "float32"),
     "o1": ("psum", [128, 512], "float32"),
 }
-SEMAPHORES = (["ld", "ldq", "one", "idn", "pa", "snt", "rc", "yy", "out"] + ["b%d" % c for c in range(NC)]
-              + ["%s%d" % (n, s) for s in range(NS) for n in ("mx", "nm", "w", "dg", "x", "la", "pv", "ev")]
-              + ["%s%d_%d" % (n, s, b) for s in range(NS) for b in range(NB) for n in ("st", "ex", "tp", "pt")])
+SEMAPHORES = (["ld", "ldq", "one", "idn", "pa", "snt", "yy", "out"] + ["b%d" % c for c in range(NC)]
+              + ["mx0", "nm0", "la0", "pv0", "ev0"]
+              + ["%s0_%d" % (n, b) for b in range(2) for n in ("st", "ex", "tp", "pt")]
+              + ["fmx", "fmA", "fmB", "fw1", "ffA", "ft1", "fa", "fb", "fc", "fpvA", "fevA", "fdg", "frc", "foa", "fob"]
+              + ["%s%d" % (n, b) for b in range(4) for n in ("fst", "fex", "ftp", "fpt")])
 
 
 def _bits(mask):
@@ -176,119 +179,146 @@ def rank_program(g, core, T, topo):
         return (0 if sender[(c, slot)][0] in sends else 1, 0 if near else 1)
 
     foreign = sorted([c for c in range(len(chips)) if c != slot], key=late)
-    stages = [[(slot, 0), (slot, 1)], [(c, h) for c in foreign for h in range(2)]]
+    fb = [(c, h) for c in foreign for h in range(2)]
     pe, dve, act = g.tensor, g.vector, g.scalar
     ST = [T.st0, T.st1, T.st2, T.st3]
     TP = [T.tpa, T.tpb]
-    OB = [T.o0, T.o1]
     X = AxisListType.X
     Exp = ActivationFunctionType.Exp
+    Copy = ActivationFunctionType.Copy
+    MUL, ADD = AluOpType.mult, AluOpType.add
 
     def col(i):
         return T.col[:, i:i + 1]
+
+    def blk(buf, i):
+        return buf[:, i * W:(i + 1) * W]
+
+    def kk(c, h):
+        return T.kv[:, kcol(c, h):kcol(c, h) + W]
+
+    def vv(c, h, a=0, b=W):
+        return T.kv[:, vcol(c, h) + a:vcol(c, h) + b]
+
 
     pe.wait_ge(sem.ld, 32)
     pe.wait_ge(sem.ldq, 16)
     pe.wait_ge(sem.pa, n1)
     pe.wait_ge(sem.idn, 1)
     dve.wait_ge(sem.idn, 1)
-    first = 0
-    for s, blocks in enumerate(stages):
-        nb = len(blocks)
-        last = s == NS - 1
-        cb = 16 * s
-        negm = col(cb + 16)
-        O = OB[s][:, 0:W]
+    O0 = T.o0[:, 0:W]
+    for b in range(2):
+        pe.matmul(ST[b][:, 0:W], T.qs[:, :], kk(slot, b), True, True).then_inc(sem["st0_%d" % b], 1)
+    for b in range(2):
+        dve.wait_ge(sem["st0_%d" % b], 1)
+        dve.tensor_reduce(col(1 + b), ST[b][:, 0:W], X, AluOpType.max, negate=True).then_inc(sem.mx0, 1)
+    dve.wait_ge(sem.mx0, 2)
+    dve.tensor_reduce(col(16), T.col[:, 1:3], X, AluOpType.min).then_inc(sem.nm0, 1)
+    act.wait_ge(sem.nm0, 1)
+    for b in range(2):
+        act.activation(blk(T.p, b), ST[b][:, 0:W], Exp, bias=col(16), scale=1.0,
+                       accum_out=col(6 + b)).then_inc(sem["ex0_%d" % b], 1)
+    for b in range(2):
+        pe.wait_ge(sem["ex0_%d" % b], 1)
+        pe.transpose(TP[b][:, 0:W], blk(T.p, b), T.idn[:, :]).then_inc(sem["tp0_%d" % b], 1)
+    for b in range(2):
+        dve.wait_ge(sem["tp0_%d" % b], 1)
+        dve.tensor_copy(blk(T.pt, b), TP[b][:, 0:W]).then_inc(sem["pt0_%d" % b], 1)
+    for b in range(2):
+        pe.wait_ge(sem["pt0_%d" % b], 1)
+        pe.matmul(O0, blk(T.pt, b), vv(slot, b), b == 0, b == 1).then_inc(sem.pv0, 1)
+    dve.wait_ge(sem["ex0_0"], 1)
+    dve.wait_ge(sem["ex0_1"], 1)
+    dve.tensor_reduce(col(11), T.col[:, 6:8], X, ADD).then_inc(sem.la0, 1)
+    dve.wait_ge(sem.pv0, 2)
+    dve.tensor_copy(T.osb[:, :], O0).then_inc(sem.ev0, 1)
 
-        def S(n, b=None, s=s):
-            return sem["%s%d" % (n, s)] if b is None else sem["%s%d_%d" % (n, s, b)]
+    OA = T.o1[:, 0:W]
+    OB = [T.o0[:, 0:H], T.st0[:, 0:H]]
 
-        def blk(buf, b, first=first):
-            return buf[:, (first + b) * W:(first + b + 1) * W]
+    for b, (c, h) in enumerate(fb):
+        if h == 0:
+            pe.wait_ge(sem["b%d" % c], sum(per_dest(x) for x in sender[(c, slot)]))
+        pe.matmul(ST[b][:, 0:W], T.qs[:, :], kk(c, h), True, True).then_inc(sem["fst%d" % b], 1)
 
-        seen = slot
-        for b, (c, h) in enumerate(blocks):
-            if c != seen:
-                pe.wait_ge(sem["b%d" % c], sum(per_dest(x) for x in sender[(c, slot)]))
-                seen = c
-            pe.matmul(ST[b][:, 0:W], T.qs[:, :], T.kv[:, kcol(c, h):kcol(c, h) + W], True, True).then_inc(
-                S("st", b), 1)
-        for b in range(nb):
-            dve.wait_ge(S("st", b), 1)
-            dve.tensor_reduce(col(cb + 1 + b), ST[b][:, 0:W], X, AluOpType.max, negate=True).then_inc(S("mx"), 1)
-        dve.wait_ge(S("mx"), nb)
-        if s > 0:
-            dve.wait_ge(sem["nm%d" % (s - 1)], 1)
-        dve.tensor_reduce(negm, T.col[:, (cb if s > 0 else cb + 1):cb + 1 + nb], X, AluOpType.min).then_inc(
-            S("nm"), 1)
-        act.wait_ge(S("nm"), 1)
-        if s > 0:
-            act.activation(col(cb + 10), col(cb), Exp, bias=negm, scale=-1.0).then_inc(S("w"), 1)
-        for b in range(nb):
-            act.activation(blk(T.p, b), ST[b][:, 0:W], Exp, bias=negm, scale=1.0,
-                           accum_out=col(cb + 6 + b)).then_inc(S("ex", b), 1)
-        if s > 0:
-            dve.wait_ge(S("w"), 1)
-            dve.tensor_scalar(T.dg[:, :], T.idn[:, :], col(cb + 10), None, AluOpType.mult).then_inc(S("dg"), 1)
-            dve.wait_ge(sem["la%d" % (s - 1)], 1)
-            dve.tensor_tensor(col(cb + 5), col(cb - 16 + 11), col(cb + 10), AluOpType.mult).then_inc(S("x"), 1)
+    for b in range(2):
+        dve.wait_ge(sem["fst%d" % b], 1)
+        dve.tensor_reduce(col(17 + b), ST[b][:, 0:W], X, AluOpType.max, negate=True).then_inc(sem.fmx, 1)
+    dve.wait_ge(sem.fmx, 2)
+    dve.wait_ge(sem.nm0, 1)
+    dve.tensor_reduce(col(19), T.col[:, 16:19], X, AluOpType.min).then_inc(sem.fmA, 1)
+    for b in range(2, 4):
+        dve.wait_ge(sem["fst%d" % b], 1)
+        dve.tensor_reduce(col(18 + b), ST[b][:, 0:W], X, AluOpType.max, negate=True).then_inc(sem.fmx, 1)
+    dve.wait_ge(sem.fmx, 4)
+    dve.wait_ge(sem.fmA, 1)
+    dve.tensor_reduce(col(22), T.col[:, 19:22], X, AluOpType.min).then_inc(sem.fmB, 1)
 
-        npv = nb
-        if s > 0:
-            pe.wait_ge(S("dg"), 1)
-            pe.wait_ge(sem["ev%d" % (s - 1)], 1)
-            pe.matmul(O, T.dg[:, :], T.osb[:, :], True, False).then_inc(S("pv"), 1)
-            npv += 1
+    act.wait_ge(sem.fmA, 1)
+    for b in range(2):
+        act.activation(blk(T.p, 2 + b), ST[b][:, 0:W], Exp, bias=col(19), scale=1.0,
+                       accum_out=col(24 + b)).then_inc(sem["fex%d" % b], 1)
+    act.activation(col(28), col(16), Exp, bias=col(19), scale=-1.0).then_inc(sem.fw1, 1)
+    act.wait_ge(sem.fmB, 1)
+    act.activation(col(29), col(19), Exp, bias=col(22), scale=-1.0).then_inc(sem.ffA, 1)
+    for b in range(2, 4):
+        act.activation(blk(T.p, 2 + b), ST[b][:, 0:W], Exp, bias=col(22), scale=1.0,
+                       accum_out=col(24 + b)).then_inc(sem["fex%d" % b], 1)
+    for b in range(2, 4):
+        act.wait_ge(sem["ftp%d" % b], 1)
+        act.activation(blk(T.pt, 2 + b), TP[b % 2][:, 0:W], Copy).then_inc(sem["fpt%d" % b], 1)
 
-        def turn(b):
-            pe.wait_ge(S("ex", b), 1)
-            if b >= 2:
-                pe.wait_ge(S("pt", b - 2), 1)
-            pe.transpose(TP[b % 2][:, 0:W], blk(T.p, b), T.idn[:, :]).then_inc(S("tp", b), 1)
+    for b in range(2):
+        pe.wait_ge(sem["fex%d" % b], 1)
+        pe.transpose(TP[b][:, 0:W], blk(T.p, 2 + b), T.idn[:, :]).then_inc(sem["ftp%d" % b], 1)
+    pe.wait_ge(sem.fpt0, 1)
+    pe.matmul(OA, blk(T.pt, 2), vv(*fb[0]), True, False)
+    pe.wait_ge(sem.fpt1, 1)
+    pe.matmul(OA, blk(T.pt, 3), vv(*fb[1]), False, True).then_inc(sem.fpvA, 1)
+    for b in range(2, 4):
+        pe.wait_ge(sem["fex%d" % b], 1)
+        pe.transpose(TP[b % 2][:, 0:W], blk(T.p, 2 + b), T.idn[:, :]).then_inc(sem["ftp%d" % b], 1)
+    pe.wait_ge(sem.ev0, 1)
+    pe.wait_ge(sem.fpt2, 1)
+    for i in range(2):
+        pe.matmul(OB[i], blk(T.pt, 4), vv(fb[2][0], fb[2][1], i * H, (i + 1) * H), True, False)
+    pe.wait_ge(sem.fpt3, 1)
+    pe.matmul(OB[0], blk(T.pt, 5), vv(fb[3][0], fb[3][1], 0, H), False, False)
+    pe.wait_ge(sem.fdg, 1)
+    pe.wait_ge(sem.fevA, 1)
+    pe.matmul(OB[0], T.dg[:, :], T.osa[:, 0:H], False, True).then_inc(sem.foa, 1)
+    pe.matmul(OB[1], blk(T.pt, 5), vv(fb[3][0], fb[3][1], H, W), False, False)
+    pe.matmul(OB[1], T.dg[:, :], T.osa[:, H:W], False, True).then_inc(sem.fob, 1)
 
-        turn(0)
-        turn(1)
-        for b, (c, h) in enumerate(blocks):
-            pe.wait_ge(S("pt", b), 1)
-            pe.matmul(O, blk(T.pt, b), T.kv[:, vcol(c, h):vcol(c, h) + W], s == 0 and b == 0,
-                      b == nb - 1).then_inc(S("pv"), 1)
-            if b + 2 < nb:
-                turn(b + 2)
+    for b in range(2):
+        dve.wait_ge(sem["ftp%d" % b], 1)
+        dve.tensor_copy(blk(T.pt, 2 + b), TP[b][:, 0:W]).then_inc(sem["fpt%d" % b], 1)
+    dve.wait_ge(sem.fw1, 1)
+    dve.wait_ge(sem.ev0, 1)
+    dve.tensor_scalar(T.t1[:, :], T.osb[:, :], col(28), None, MUL).then_inc(sem.ft1, 1)
+    dve.wait_ge(sem.la0, 1)
+    dve.wait_ge(sem.fex0, 1)
+    dve.tensor_scalar(col(33), col(11), col(28), col(24), MUL, ADD).then_inc(sem.fa, 1)
+    dve.wait_ge(sem.fa, 1)
+    dve.wait_ge(sem.fex1, 1)
+    dve.wait_ge(sem.ffA, 1)
+    dve.tensor_scalar(col(34), col(33), col(25), col(29), ADD, MUL).then_inc(sem.fb, 1)
+    dve.wait_ge(sem.fpvA, 1)
+    dve.wait_ge(sem.ft1, 1)
+    dve.tensor_tensor(T.osa[:, :], OA, T.t1[:, :], ADD).then_inc(sem.fevA, 1)
+    dve.tensor_scalar(T.dg[:, :], T.idn[:, :], col(29), None, MUL).then_inc(sem.fdg, 1)
+    dve.wait_ge(sem.fb, 1)
+    dve.wait_ge(sem.fex2, 1)
+    dve.wait_ge(sem.fex3, 1)
+    dve.tensor_scalar(col(31), col(34), col(26), col(27), ADD, ADD).then_inc(sem.fc, 1)
+    dve.wait_ge(sem.fc, 1)
+    dve.reciprocal(col(32), col(31)).then_inc(sem.frc, 1)
+    dve.wait_ge(sem.frc, 1)
+    dve.wait_ge(sem.foa, 1)
+    dve.tensor_scalar(T.ys[:, 0:H], OB[0], col(32), None, MUL).then_inc(sem.yy, 1)
+    dve.wait_ge(sem.fob, 1)
+    dve.tensor_scalar(T.ys[:, H:W], OB[1], col(32), None, MUL).then_inc(sem.yy, 1)
 
-        def copy(b):
-            dve.wait_ge(S("tp", b), 1)
-            dve.tensor_copy(blk(T.pt, b), TP[b % 2][:, 0:W]).then_inc(S("pt", b), 1)
-
-        def rowsum():
-            for b in range(nb):
-                dve.wait_ge(S("ex", b), 1)
-            if s > 0:
-                dve.wait_ge(S("x"), 1)
-            dve.tensor_reduce(col(cb + 11), T.col[:, (cb + 5 if s > 0 else cb + 6):cb + 6 + nb], X,
-                              AluOpType.add).then_inc(S("la"), 1)
-
-        def recip():
-            dve.wait_ge(S("la"), 1)
-            dve.reciprocal(col(cb + 12), col(cb + 11)).then_inc(sem.rc, 1)
-
-        if not last:
-            for b in range(nb):
-                copy(b)
-            rowsum()
-            dve.wait_ge(S("pv"), npv)
-            dve.tensor_copy(T.osb[:, :], O).then_inc(S("ev"), 1)
-        else:
-            for b in range(nb - 2):
-                copy(b)
-            rowsum()
-            copy(nb - 2)
-            recip()
-            copy(nb - 1)
-            dve.wait_ge(sem.rc, 1)
-            dve.wait_ge(S("pv"), npv)
-            dve.tensor_scalar(T.ys[:, :], O, col(cb + 12), None, AluOpType.mult).then_inc(sem.yy, 1)
-        first += nb
-
-    g.sync.wait_ge(sem.yy, 1)
+    g.sync.wait_ge(sem.yy, 2)
     g.sync.dma_start(T.y[:, :], T.ys[:, :]).then_inc(sem.out, 16)
     g.sync.wait_ge(sem.out, 16)

from concourse.bass import DstId, RemoteDMATransfer
from concourse.mybir import AluOpType, AxisListType, ActivationFunctionType

NC = 3
W = 128
H = 64
NCORES = 80

SCRATCH = {
    "kv": ("sbuf", [128, NC * 4 * W], "bfloat16"),
    "qs": ("sbuf", [128, W], "bfloat16"),
    "ones": ("sbuf", [128, W], "bfloat16"),
    "idn": ("sbuf", [128, W], "bfloat16"),
    "p": ("sbuf", [128, NC * 2 * W], "bfloat16"),
    "pt": ("sbuf", [128, NC * 2 * W], "bfloat16"),
    "dg": ("sbuf", [128, W], "bfloat16"),
    "osb": ("sbuf", [128, W], "bfloat16"),
    "t1": ("sbuf", [128, W], "bfloat16"),
    "osa": ("sbuf", [128, W], "bfloat16"),
    "col": ("sbuf", [128, 48], "float32"),
    "ys": ("sbuf", [128, W], "bfloat16"),
    "st0": ("psum", [128, 512], "float32"),
    "st1": ("psum", [128, 512], "float32"),
    "st2": ("psum", [128, 512], "float32"),
    "st3": ("psum", [128, 512], "float32"),
    "tpa": ("psum", [128, 1024], "bfloat16"),
    "tpb": ("psum", [128, 1024], "bfloat16"),
    "o0": ("psum", [128, 512], "float32"),
    "o1": ("psum", [128, 512], "float32"),
}
SEMAPHORES = (["ld", "ldq", "one", "idn", "pa", "snt", "yy", "out"] + ["b%d" % c for c in range(NC)]
              + ["mx0", "nm0", "la0", "pv0", "ev0"]
              + ["%s0_%d" % (n, b) for b in range(2) for n in ("st", "ex", "tp", "pt")]
              + ["fmx", "fmA", "fmB", "fw1", "ffA", "ft1", "fa", "fb", "fc", "fpvA", "fevA", "fdg", "frc", "foa", "fob"]
              + ["%s%d" % (n, b) for b in range(4) for n in ("fst", "fex", "ftp", "fpt")])


def _bits(mask):
    return [e for e in range(mask.bit_length()) if (mask >> e) & 1]


def _mask(engs):
    m = 0
    for e in engs:
        m |= 1 << e
    return m


def _common(x, T, topo):
    m = -1
    for d in T.cores:
        if d != x:
            m = topo.mask(x, d) if m < 0 else m & topo.mask(x, d)
    return _bits(m)


def _plan(T, topo):
    cores = list(T.cores)
    chips = []
    for c in cores:
        if topo.chip(c) not in chips:
            chips.append(topo.chip(c))
    members = [[c for c in cores if topo.chip(c) == ch] for ch in chips]
    jobs = []
    for a in range(len(chips)):
        for b in range(len(chips)):
            if a != b:
                elig = [c for c in members[a] if all(topo.may_write(c, d) for d in members[b])]
                near = topo.mates(chips[a], chips[b]) or topo.same_plane(chips[a], chips[b])
                jobs.append((len(elig), 1 if near else 0, a, b, elig))
    jobs.sort(key=lambda j: j[:4])
    sends = {c: [] for c in cores}
    relay = {}
    feeds = {c: [] for c in cores}
    sender = {}
    for _, _, a, b, elig in jobs:
        s = min(elig, key=lambda c: len(sends[c]))
        if sends[s]:
            free = [c for c in range(NCORES) if topo.chip(c) == chips[a] and c not in cores and c not in relay
                    and all(topo.may_write(c, d) for d in members[b])]
            free.sort(key=lambda c: (topo.die(c) == topo.die(s), c))
            free = free[:len(members[a])]
            if len(free) == len(members[a]):
                for owner, h in zip(members[a], free):
                    relay[h] = (owner, members[b])
                    feeds[owner] = feeds[owner] + [h]
                sender[(a, b)] = free
                continue
        sends[s] = sends[s] + members[b]
        sender[(a, b)] = [s]
    return chips, members, sends, sender, relay, feeds


def _step1(x, partner, feeds, T, topo):
    dests = [partner] + feeds[x]
    eng = _common(x, T, topo)
    m = topo.mask(x, partner)
    for d in dests:
        m &= topo.mask(x, d)
    pool = eng + [e for e in _bits(m) if e not in eng]
    per = 1
    while per * 2 * len(dests) <= len(pool) and per * 2 <= len(eng):
        per *= 2
    return [(d, pool[i * per:(i + 1) * per]) for i, d in enumerate(dests)]


def rank_program(g, core, T, topo):
    rank = T.rank_of(core)
    sem = T.sem
    chips, members, sends, sender, relay, feeds = _plan(T, topo)

    def place(c):
        s = chips.index(topo.chip(c))
        return s, members[s].index(c)

    def per_dest(x):
        return len(_common(x, T, topo)) // len(sends[x] if x in sends else relay[x][1])

    def cross(dests, c0, c1, bsem):
        eng = _common(core, T, topo)
        per = per_dest(core)
        trs = []
        for i, d in enumerate(dests):
            rid, pid, _ = topo.addr(d)
            trs.append(RemoteDMATransfer(dst_ids=[DstId(rid=rid, pnc=pid)],
                                         dma_engine_mask=_mask(eng[i * per:(i + 1) * per]), remote_sem=bsem,
                                         src=T.kv[:, c0:c1], dst=T.kv[:, c0:c1]))
        g.remote_dma_fused(trs, local_sem=sem.snt)
        return per * len(dests)

    if rank is None:
        if core in relay:
            owner, dests = relay[core]
            oslot, opos = place(owner)
            got = [e for d, e in _step1(owner, members[oslot][1 - opos], feeds, T, topo) if d == core][0]
            h0 = oslot * 4 * W + opos * 2 * W
            g.wait_ge(sem.pa, len(got))
            g.wait_ge(sem.snt, cross(dests, h0, h0 + 2 * W, sem["b%d" % oslot]))
        return

    slot, pos = place(core)
    partner = members[slot][1 - pos]

    def kcol(c, b):
        return c * 4 * W + W + b * W

    def vcol(c, b):
        return c * 4 * W + 3 * b * W

    n1 = len(_step1(partner, core, feeds, T, topo)[0][1])

    g.sync.dma_start(T.kv[:, kcol(slot, pos):kcol(slot, pos) + W], T.k[:, :]).then_inc(sem.ld, 16)
    g.scalar.dma_start(T.kv[:, vcol(slot, pos):vcol(slot, pos) + W], T.v[:, :]).then_inc(sem.ld, 16)
    g.sync.dma_start(T.qs[:, :], T.q[:, :]).then_inc(sem.ldq, 16)

    g.vector.memset(T.ones[:, :], 1.0).then_inc(sem.one, 1)
    g.wait_ge(sem.one, 1)
    g.affine_select(T.idn[:, :], T.ones[:, :], [[-1, W]], AluOpType.is_equal, 0.0, 0, 1).then_inc(sem.idn, 1)

    h0 = slot * 4 * W + pos * 2 * W
    g.wait_ge(sem.ld, 32)
    trs = []
    sent = 0
    for d, engs in _step1(core, partner, feeds, T, topo):
        rid, pid, _ = topo.addr(d)
        trs.append(RemoteDMATransfer(dst_ids=[DstId(rid=rid, pnc=pid)], dma_engine_mask=_mask(engs),
                                     remote_sem=sem.pa, src=T.kv[:, h0:h0 + 2 * W], dst=T.kv[:, h0:h0 + 2 * W]))
        sent += len(engs)
    g.remote_dma_fused(trs, local_sem=sem.snt)

    if sends[core]:
        g.wait_ge(sem.pa, n1)
        b0 = slot * 4 * W
        sent += cross(sends[core], b0, b0 + 4 * W, sem["b%d" % slot])
    g.wait_ge(sem.snt, sent)

    def late(c):
        near = topo.mates(chips[c], chips[slot]) or topo.same_plane(chips[c], chips[slot])
        return (0 if sender[(c, slot)][0] in sends else 1, 0 if near else 1)

    foreign = sorted([c for c in range(len(chips)) if c != slot], key=late)
    fb = [(c, h) for c in foreign for h in range(2)]
    pe, dve, act = g.tensor, g.vector, g.scalar
    ST = [T.st0, T.st1, T.st2, T.st3]
    TP = [T.tpa, T.tpb]
    X = AxisListType.X
    Exp = ActivationFunctionType.Exp
    Copy = ActivationFunctionType.Copy
    MUL, ADD = AluOpType.mult, AluOpType.add

    def col(i):
        return T.col[:, i:i + 1]

    def blk(buf, i):
        return buf[:, i * W:(i + 1) * W]

    def kk(c, h):
        return T.kv[:, kcol(c, h):kcol(c, h) + W]

    def vv(c, h, a=0, b=W):
        return T.kv[:, vcol(c, h) + a:vcol(c, h) + b]


    pe.wait_ge(sem.ld, 32)
    pe.wait_ge(sem.ldq, 16)
    pe.wait_ge(sem.pa, n1)
    pe.wait_ge(sem.idn, 1)
    dve.wait_ge(sem.idn, 1)
    O0 = T.o0[:, 0:W]
    for b in range(2):
        pe.matmul(ST[b][:, 0:W], T.qs[:, :], kk(slot, b), True, True).then_inc(sem["st0_%d" % b], 1)
    for b in range(2):
        dve.wait_ge(sem["st0_%d" % b], 1)
        dve.tensor_reduce(col(1 + b), ST[b][:, 0:W], X, AluOpType.max, negate=True).then_inc(sem.mx0, 1)
    dve.wait_ge(sem.mx0, 2)
    dve.tensor_reduce(col(16), T.col[:, 1:3], X, AluOpType.min).then_inc(sem.nm0, 1)
    act.wait_ge(sem.nm0, 1)
    for b in range(2):
        act.activation(blk(T.p, b), ST[b][:, 0:W], Exp, bias=col(16), scale=1.0,
                       accum_out=col(6 + b)).then_inc(sem["ex0_%d" % b], 1)
    for b in range(2):
        pe.wait_ge(sem["ex0_%d" % b], 1)
        pe.transpose(TP[b][:, 0:W], blk(T.p, b), T.idn[:, :]).then_inc(sem["tp0_%d" % b], 1)
    for b in range(2):
        dve.wait_ge(sem["tp0_%d" % b], 1)
        dve.tensor_copy(blk(T.pt, b), TP[b][:, 0:W]).then_inc(sem["pt0_%d" % b], 1)
    for b in range(2):
        pe.wait_ge(sem["pt0_%d" % b], 1)
        pe.matmul(O0, blk(T.pt, b), vv(slot, b), b == 0, b == 1).then_inc(sem.pv0, 1)
    dve.wait_ge(sem["ex0_0"], 1)
    dve.wait_ge(sem["ex0_1"], 1)
    dve.tensor_reduce(col(11), T.col[:, 6:8], X, ADD).then_inc(sem.la0, 1)
    dve.wait_ge(sem.pv0, 2)
    dve.tensor_copy(T.osb[:, :], O0).then_inc(sem.ev0, 1)

    OA = T.o1[:, 0:W]
    OB = [T.o0[:, 0:H], T.st0[:, 0:H]]

    for b, (c, h) in enumerate(fb):
        if h == 0:
            pe.wait_ge(sem["b%d" % c], sum(per_dest(x) for x in sender[(c, slot)]))
        pe.matmul(ST[b][:, 0:W], T.qs[:, :], kk(c, h), True, True).then_inc(sem["fst%d" % b], 1)

    for b in range(2):
        dve.wait_ge(sem["fst%d" % b], 1)
        dve.tensor_reduce(col(17 + b), ST[b][:, 0:W], X, AluOpType.max, negate=True).then_inc(sem.fmx, 1)
    dve.wait_ge(sem.fmx, 2)
    dve.wait_ge(sem.nm0, 1)
    dve.tensor_reduce(col(19), T.col[:, 16:19], X, AluOpType.min).then_inc(sem.fmA, 1)
    for b in range(2, 4):
        dve.wait_ge(sem["fst%d" % b], 1)
        dve.tensor_reduce(col(18 + b), ST[b][:, 0:W], X, AluOpType.max, negate=True).then_inc(sem.fmx, 1)
    dve.wait_ge(sem.fmx, 4)
    dve.wait_ge(sem.fmA, 1)
    dve.tensor_reduce(col(22), T.col[:, 19:22], X, AluOpType.min).then_inc(sem.fmB, 1)

    act.wait_ge(sem.fmA, 1)
    for b in range(2):
        act.activation(blk(T.p, 2 + b), ST[b][:, 0:W], Exp, bias=col(19), scale=1.0,
                       accum_out=col(24 + b)).then_inc(sem["fex%d" % b], 1)
    act.activation(col(28), col(16), Exp, bias=col(19), scale=-1.0).then_inc(sem.fw1, 1)
    act.wait_ge(sem.fmB, 1)
    act.activation(col(29), col(19), Exp, bias=col(22), scale=-1.0).then_inc(sem.ffA, 1)
    for b in range(2, 4):
        act.activation(blk(T.p, 2 + b), ST[b][:, 0:W], Exp, bias=col(22), scale=1.0,
                       accum_out=col(24 + b)).then_inc(sem["fex%d" % b], 1)
    for b in range(2, 4):
        act.wait_ge(sem["ftp%d" % b], 1)
        act.activation(blk(T.pt, 2 + b), TP[b % 2][:, 0:W], Copy).then_inc(sem["fpt%d" % b], 1)

    for b in range(2):
        pe.wait_ge(sem["fex%d" % b], 1)
        pe.transpose(TP[b][:, 0:W], blk(T.p, 2 + b), T.idn[:, :]).then_inc(sem["ftp%d" % b], 1)
    pe.wait_ge(sem.fpt0, 1)
    pe.matmul(OA, blk(T.pt, 2), vv(*fb[0]), True, False)
    pe.wait_ge(sem.fpt1, 1)
    pe.matmul(OA, blk(T.pt, 3), vv(*fb[1]), False, True).then_inc(sem.fpvA, 1)
    for b in range(2, 4):
        pe.wait_ge(sem["fex%d" % b], 1)
        pe.transpose(TP[b % 2][:, 0:W], blk(T.p, 2 + b), T.idn[:, :]).then_inc(sem["ftp%d" % b], 1)
    pe.wait_ge(sem.ev0, 1)
    pe.wait_ge(sem.fpt2, 1)
    for i in range(2):
        pe.matmul(OB[i], blk(T.pt, 4), vv(fb[2][0], fb[2][1], i * H, (i + 1) * H), True, False)
    pe.wait_ge(sem.fpt3, 1)
    pe.matmul(OB[0], blk(T.pt, 5), vv(fb[3][0], fb[3][1], 0, H), False, False)
    pe.wait_ge(sem.fdg, 1)
    pe.wait_ge(sem.fevA, 1)
    pe.matmul(OB[0], T.dg[:, :], T.osa[:, 0:H], False, True).then_inc(sem.foa, 1)
    pe.matmul(OB[1], blk(T.pt, 5), vv(fb[3][0], fb[3][1], H, W), False, False)
    pe.matmul(OB[1], T.dg[:, :], T.osa[:, H:W], False, True).then_inc(sem.fob, 1)

    for b in range(2):
        dve.wait_ge(sem["ftp%d" % b], 1)
        dve.tensor_copy(blk(T.pt, 2 + b), TP[b][:, 0:W]).then_inc(sem["fpt%d" % b], 1)
    dve.wait_ge(sem.fw1, 1)
    dve.wait_ge(sem.ev0, 1)
    dve.tensor_scalar(T.t1[:, :], T.osb[:, :], col(28), None, MUL).then_inc(sem.ft1, 1)
    dve.wait_ge(sem.la0, 1)
    dve.wait_ge(sem.fex0, 1)
    dve.tensor_scalar(col(33), col(11), col(28), col(24), MUL, ADD).then_inc(sem.fa, 1)
    dve.wait_ge(sem.fa, 1)
    dve.wait_ge(sem.fex1, 1)
    dve.wait_ge(sem.ffA, 1)
    dve.tensor_scalar(col(34), col(33), col(25), col(29), ADD, MUL).then_inc(sem.fb, 1)
    dve.wait_ge(sem.fpvA, 1)
    dve.wait_ge(sem.ft1, 1)
    dve.tensor_tensor(T.osa[:, :], OA, T.t1[:, :], ADD).then_inc(sem.fevA, 1)
    dve.tensor_scalar(T.dg[:, :], T.idn[:, :], col(29), None, MUL).then_inc(sem.fdg, 1)
    dve.wait_ge(sem.fb, 1)
    dve.wait_ge(sem.fex2, 1)
    dve.wait_ge(sem.fex3, 1)
    dve.tensor_scalar(col(31), col(34), col(26), col(27), ADD, ADD).then_inc(sem.fc, 1)
    dve.wait_ge(sem.fc, 1)
    dve.reciprocal(col(32), col(31)).then_inc(sem.frc, 1)
    dve.wait_ge(sem.frc, 1)
    dve.wait_ge(sem.foa, 1)
    dve.tensor_scalar(T.ys[:, 0:H], OB[0], col(32), None, MUL).then_inc(sem.yy, 1)
    dve.wait_ge(sem.fob, 1)
    dve.tensor_scalar(T.ys[:, H:W], OB[1], col(32), None, MUL).then_inc(sem.yy, 1)

    g.sync.wait_ge(sem.yy, 2)
    g.sync.dma_start(T.y[:, :], T.ys[:, :]).then_inc(sem.out, 16)
    g.sync.wait_ge(sem.out, 16)
